import numpy as np
import ml_dtypes


def mxq(x, axis, fmt="e4m3"):
    dtype, down = {"e4m3": (ml_dtypes.float8_e4m3fn, 7), "e5m2": (ml_dtypes.float8_e5m2, 14)}[fmt]
    v = np.moveaxis(np.asarray(x, np.float32).astype(ml_dtypes.bfloat16).astype(np.float64), axis, -1)
    blocks = v.reshape(v.shape[:-1] + (-1, 32))
    amax = np.abs(blocks).max(-1, keepdims=True)
    byte = np.maximum(np.where(amax > 0, np.frexp(amax)[1] - 1 + 127, 0) - down, 1)
    scale = np.exp2(byte - 127.0)
    codes = (blocks / scale).astype(np.float32).astype(dtype).astype(np.float64)
    return np.moveaxis((codes * scale).reshape(v.shape), -1, axis)


WIDE = False


def mx_kscale(k):
    if not WIDE:
        return np.ones(k)
    levels = np.array([10, -10, 5, -5, 0])
    if k % 512:
        return np.exp2(np.random.permutation(np.resize(levels, k // 32))).repeat(32)
    a = np.empty((k // 512, 16))
    for p in range(k // 512):
        a[p, :8] = np.random.permutation(np.resize(levels, 8))
        for g in range(8):
            far = levels[np.abs(levels - a[p, g]) >= 10]
            a[p, g + 8] = far[np.random.randint(len(far))]
    return np.exp2(a.ravel()).repeat(32)


def f64(x):
    return np.asarray(x).astype(np.float64)


def striped(idx):
    return np.tile(idx.reshape(-1, 16).T, (8, 1)).astype(np.uint16)


def unstriped(offs):
    return offs[:16].T.reshape(-1).astype(np.int64)


def striped8(idx):
    return np.concatenate([x.reshape(-1, 16).T for x in idx]).astype(np.uint16)


def runs(offs, k):
    lists = np.stack([offs[16 * r : 16 * r + 16].T.reshape(-1) for r in range(8)]).astype(np.int64)
    return lists[np.arange(k) % 512 // 64]


def pack_weight(w):
    k, n = w.shape
    w = f64(np.asarray(w, np.float32).astype(ml_dtypes.bfloat16)).reshape(k // 32, 32, n)
    amax = np.abs(w).max(1)
    byte = np.clip(np.where(amax > 0, np.frexp(amax)[1] - 1 + 127 - 7, 1), 1, 254)
    scaled = (w * np.exp2(127.0 - byte)[:, None, :]).reshape(k, n).astype(np.float32)
    words = np.ascontiguousarray(scaled.reshape(k // 512, 128, 4, n).transpose(0, 1, 3, 2)).astype(ml_dtypes.float8_e4m3fn).view(np.uint8)
    return words, np.ascontiguousarray(byte.astype(np.uint8).reshape(k // 512, 16, n))


def unpack_weight(words, scales):
    g, p, n, _ = words.shape
    vals = np.ascontiguousarray(words).view(ml_dtypes.float8_e4m3fn).astype(np.float64) * np.repeat(np.exp2(scales.astype(np.float64) - 127.0), 8, axis=1)[..., None]
    return vals.transpose(0, 1, 3, 2).reshape(g * 512, n)


K, T, S, N, H = 512, 2048, 512, 512, 512


def setup_inputs():
    n = np.random.standard_normal
    s = mx_kscale(K)[:, None]
    u = mx_kscale(H)
    packed_xT = pack_weight(n((K, T)) * s)
    return {
        "x_words": packed_xT[0],
        "x_scales": packed_xT[1],
        "w1": (n((K, H)) / np.sqrt(K) / s).astype(np.float32),
        "gn": (np.random.uniform(0.5, 1.5, (H, 1)) * u[:, None]).astype(np.float32),
        "w2": (n((H, N)) / np.sqrt(2 * H) / u[:, None]).astype(np.float32),
        "w3": (n((K, N)) / np.sqrt(2 * K) / s).astype(np.float32),
        "offs": striped(np.random.permutation(T)[:S]),
        "n1": striped(np.random.permutation(S)),
        "hz": striped8(np.random.randint(0, T, (8, S))),
        "n2": striped(np.random.permutation(S)),
        "n3": striped(np.random.permutation(S)),
    }


def reference(x_words, x_scales, w1, gn, w2, w3, offs, n1, hz, n2, n3):
    xq = unpack_weight(x_words, x_scales)[:, unstriped(offs)]
    y = mxq(f64(w1), 0, "e4m3").T @ xq
    z = f64(gn) * (y / (np.abs(y[:, unstriped(n1)]) + 0.5))
    x_hz = unpack_weight(x_words, x_scales)[np.arange(K)[:, None], runs(hz, K)]
    h = mxq(f64(w2), 0, "e4m3").T @ mxq(z, 0, "e4m3") + mxq(f64(w3), 0, "e4m3").T @ x_hz
    pa = h[:, unstriped(n2)]
    kr = np.exp(-0.5 * ((h - pa) ** 2))
    pb = h[:, unstriped(n3)]
    kr2 = np.exp(-0.5 * ((h - pb) ** 2))
    return (kr * pa + kr2 * pb) / (kr + kr2 + 0.5)

@@ -1,0 +1,207 @@
+from contextlib import ExitStack
+
+import concourse.mybir as mybir
+
+K, T, S, N, H = 512, 2048, 512, 512, 512
+FLOPS = 2 * S * (K * H + H * N + K * N)
+
+F32 = mybir.dt.float32
+BF16 = mybir.dt.bfloat16
+I32 = mybir.dt.int32
+U32 = mybir.dt.uint32
+U16 = mybir.dt.uint16
+U8 = mybir.dt.uint8
+FP8X4 = mybir.dt.float8_e4m3fn_x4
+ACT = mybir.ActivationFunctionType
+ALU = mybir.AluOpType
+
+P = 128
+PACK = 4
+HALF = S // 2
+Z_CHUNKS = ((0, 256), (256, 384), (384, 512))
+
+
+def tile_picked_mixhnormkern_none_p_kernel(tc, x_words, x_scales, w1, gn, w2, w3, offs, n1, hz, n2, n3, out):
+    nc = tc.nc
+    with ExitStack() as ctx:
+        keep = ctx.enter_context(tc.tile_pool(name="keep", bufs=1))
+        psum = ctx.enter_context(tc.psum_pool(name="psum", bufs=1))
+
+        def sb(name, shape, dtype, tag=None):
+            return keep.tile(shape, dtype, name=name, tag=tag or name, align_bytes=64)
+
+        def load_list(name, src):
+            tile = sb(name, [P, S // 16], U16)
+            nc.sync.dma_start(tile[:], src)
+            return tile
+
+        def entries(lst, lo, hi):
+            return lst[:, lo // 16 : hi // 16]
+
+        xs = sb("xs", [P, T], U8)
+        nc.vector.memset(xs[:].bitcast(I32), 0)
+        scale_rows = x_scales[0].bitcast(I32)
+        xs8 = sb("xs8", [P, T], U8)
+        nc.vector.memset(xs8[:].bitcast(I32), 0)
+        xh_s = sb("xh_s", [P, S], U8)
+        nc.vector.memset(xh_s[:].bitcast(I32), 0)
+        offs_l = load_list("offs_l", offs)
+        hz_l = load_list("hz_l", hz)
+        n1_l = load_list("n1_l", n1)
+        n2_l = load_list("n2_l", n2)
+        n3_l = load_list("n3_l", n3)
+        gain = sb("gain", [P, PACK], F32)
+        nc.sync.dma_start(gain[:], gn.rearrange("(p t) o -> p (t o)", t=PACK))
+        xw = sb("xw", [P, T], U32)
+        nc.sync.dma_start(xw[:].bitcast(I32), x_words[0].rearrange("p n t -> p (n t)").bitcast(I32))
+        for r in range(4):
+            nc.scalar.dma_start(xs[r:P:32, :].bitcast(I32), scale_rows[r:16:4, :])
+        nc.scalar.dma_start(xs8[0:P:8, :].bitcast(I32), scale_rows)
+        w1_rows = w1.rearrange("(p j) c -> p j c", j=PACK)
+        w1_raw = []
+        for c in range(2):
+            raw = sb(f"w1_raw{c}", [P, PACK, HALF], F32)
+            nc.sync.dma_start(raw[:], w1_rows[:, :, c * HALF : (c + 1) * HALF])
+            w1_raw.append(raw)
+
+        half = sb("half", [P, 1], F32)
+        nc.vector.memset(half[:], 0.5)
+
+        xq_s = sb("xq_s", [P, S], U8)
+        nc.vector.tensor_copy(xq_s[:], xs[:].indirect(offs_l[:]))
+        xq_w = sb("xq_w", [P, S], U32)
+        nc.vector.tensor_copy(xq_w[:], xw[:].indirect(offs_l[:]))
+        xh_w = sb("xh_w", [P, S], U32)
+        nc.vector.tensor_copy(xh_w[:], xw[:].indirect(hz_l[:]))
+
+        w1_b = sb("w1_b", [P, H * PACK], BF16)
+        w1_dst = w1_b[:].rearrange("p (t m j) -> p m t j", t=PACK, j=PACK)
+        for c in range(2):
+            src = w1_raw[c][:].rearrange("p j (m t) -> p m t j", t=PACK)
+            dst = w1_dst[:, c * 64 : (c + 1) * 64]
+            if c == 0:
+                nc.scalar.copy(dst, src)
+            else:
+                nc.vector.tensor_copy(dst, src)
+        w3_raw = sb("w3_raw", [P, PACK, N], F32, tag="w1_raw0")
+        nc.sync.dma_start(w3_raw[:], w3.rearrange("(p j) c -> p j c", j=PACK))
+        w2_raw = sb("w2_raw", [P, PACK, N], F32, tag="w1_raw1")
+        nc.sync.dma_start(w2_raw[:], w2.rearrange("(p j) c -> p j c", j=PACK))
+        w1_c = sb("w1_c", [P, H], U32)
+        w1_s = sb("w1_s", [P, H], U8)
+        y = [psum.tile([P, S], F32, name=f"y{t}") for t in range(PACK)]
+        for t in range(PACK):
+            m = slice(t * P, (t + 1) * P)
+            nc.vector.quantize_mx(out=w1_c[:, m].bitcast(FP8X4), scales=w1_s[:, m], in_=w1_b[:, t * P * PACK : (t + 1) * P * PACK])
+            nc.tensor.matmul_mx(out=y[t][:], lhsT=w1_c[:, m].bitcast(FP8X4), lhsT_scale=w1_s[:, m],
+                                rhs=xq_w[:].bitcast(FP8X4), rhs_scale=xq_s[:], start=True, stop=True)
+
+        xh_raw = sb("xh_raw", [P, S], U8, tag="w1_b")
+        nc.vector.tensor_copy(xh_raw[:], xs8[:].indirect(hz_l[:]))
+        for r in range(4):
+            nc.sync.dma_start(xh_s[r:P:32, :].bitcast(I32), xh_raw[8 * r : P : 32, :].bitcast(I32))
+
+        def group_weight(name, raw, engine):
+            grouped = sb(name + "_b", [P, N, PACK], BF16)
+            dst = grouped[:].rearrange("p (c i) j -> p c j i", i=4)
+            src = raw[:].rearrange("p j (c i) -> p c j i", i=4)
+            if engine == "gpsimd":
+                nc.gpsimd.tensor_scalar(dst, src, 1.0, 0.0, ALU.mult, ALU.add)
+            else:
+                nc.vector.tensor_copy(dst, src)
+            return grouped
+
+        def quantise_weight(name, grouped):
+            codes = sb(name + "_c", [P, N], U32)
+            scales = sb(name + "_s", [P, N], U8)
+            nc.vector.quantize_mx(out=codes[:].bitcast(FP8X4), scales=scales[:], in_=grouped[:].rearrange("p c j -> p (c j)"))
+            return codes, scales
+
+        mag = sb("mag", [P, PACK, S], F32)
+        root = sb("root", [P, PACK, S], F32)
+        inv = [sb(f"inv{t}", [P, S], F32) for t in range(PACK)]
+        w3_b = group_weight("w3", w3_raw, "vector")
+        for t in range(PACK):
+            nc.scalar.activation(mag[:, t, :], y[t][:], ACT.Abs)
+            nc.scalar.activation(root[:, t, :], mag[:, t, :], ACT.Abs_reciprocal_sqrt, bias=half[:])
+            if t in (2, 3):
+                nc.scalar.activation(inv[t][:], root[:, t, :], ACT.Square)
+            else:
+                nc.vector.tensor_tensor(inv[t][:], root[:, t, :], root[:, t, :], ALU.mult)
+        w3_c, w3_s = quantise_weight("w3", w3_b)
+        h = [psum.tile([P, S], F32, name=f"h{m}") for m in range(N // P)]
+        for mt in range(N // P):
+            m = slice(mt * P, (mt + 1) * P)
+            nc.tensor.matmul_mx(out=h[mt][:], lhsT=w3_c[:, m].bitcast(FP8X4), lhsT_scale=w3_s[:, m],
+                                rhs=xh_w[:].bitcast(FP8X4), rhs_scale=xh_s[:], start=True, stop=False)
+        w2_c, w2_s = quantise_weight("w2", group_weight("w2", w2_raw, "vector"))
+
+        z_c = sb("z_c", [P, S], U32)
+        z_s = sb("z_s", [P, S], U8)
+        for lo, hi in Z_CHUNKS:
+            z_planes = sb(f"z_planes{lo}", [P, PACK, hi - lo], BF16)
+            for t in range(PACK):
+                got = sb(f"got{lo}_{t}", [P, hi - lo], F32)
+                nc.scalar.activation(got[:], inv[t][:].indirect(entries(n1_l, lo, hi)), ACT.Copy)
+                nc.vector.scalar_tensor_tensor(z_planes[:, t, :], y[t][:, lo:hi], gain[:, t : t + 1], got[:], ALU.mult, ALU.mult)
+            z_b = sb(f"z_b{lo}", [P, hi - lo, PACK], BF16)
+            nc.vector.tensor_copy(z_b[:].rearrange("p (c i) j -> p c j i", i=4), z_planes[:].rearrange("p j (c i) -> p c j i", i=4))
+            nc.vector.quantize_mx(out=z_c[:, lo:hi].bitcast(FP8X4), scales=z_s[:, lo:hi], in_=z_b[:].rearrange("p c j -> p (c j)"))
+            for mt in range(N // P):
+                m = slice(mt * P, (mt + 1) * P)
+                nc.tensor.matmul_mx(out=h[mt][:, lo:hi], lhsT=w2_c[:, m].bitcast(FP8X4), lhsT_scale=w2_s[:, m],
+                                    rhs=z_c[:, lo:hi].bitcast(FP8X4), rhs_scale=z_s[:, lo:hi], start=False, stop=(hi == S))
+
+        hs = [sb(f"hs{mt}", [P, S], F32) for mt in range(N // P)]
+        nc.scalar.copy(hs[0][:], h[0][:])
+        for mt in range(1, N // P):
+            nc.vector.tensor_copy(hs[mt][:], h[mt][:])
+        units = [(mt, c * HALF) for mt in range(N // P) for c in range(2)]
+        pab = [sb(f"pab{u}", [P, 2, HALF], F32) for u in range(len(units))]
+        dif = [sb(f"dif{u}", [P, 2, HALF], F32) for u in range(len(units))]
+        sq = [sb(f"sq{u}", [P, 4, P], F32)[:] for u in range(len(units) - 1)]
+        rden = sb("rden", [P, N // P, S], F32)
+        sq.append(rden[:, :, 0:P])
+        kr = [sb(f"kr{u}", [P, 2, HALF], F32) for u in range(len(units))]
+        den = sb("den", [P, len(units), HALF], F32)
+        num = sb("num", [P, len(units), HALF], F32)
+
+        def fetch(u):
+            mt, lo = units[u]
+            for i, lst in enumerate((n2_l, n3_l)):
+                nc.scalar.activation(pab[u][:, i, :], hs[mt][:].indirect(entries(lst, lo, lo + HALF)), ACT.Copy)
+
+        def differ(u):
+            mt, lo = units[u]
+            nc.vector.tensor_tensor(dif[u][:], pab[u][:], hs[mt][:, lo : lo + HALF].unsqueeze(1).to_broadcast([P, 2, HALF]), ALU.subtract)
+
+        def square(u):
+            d4 = dif[u][:].rearrange("p i (a c) -> p (i a) c", a=2)
+            nc.vector.tensor_tensor(sq[u], d4, d4, ALU.mult)
+
+        def weigh(u):
+            nc.scalar.activation(kr[u][:].rearrange("p i (a c) -> p (i a) c", a=2), sq[u], ACT.Exp, scale=-0.5)
+
+        def total(u):
+            nc.vector.scalar_tensor_tensor(den[:, u, :], kr[u][:, 0, :], 0.5, kr[u][:, 1, :], ALU.add, ALU.add)
+
+        stages = (fetch, differ, square, weigh, total)
+        for step in range(len(units) + len(stages) - 1):
+            for lag, stage in enumerate(stages):
+                if 0 <= step - lag < len(units):
+                    stage(step - lag)
+
+        num_rows = num[:].rearrange("p u c -> p (u c)")
+        den_rows = den[:].rearrange("p u c -> p (u c)")
+        for mt in range(N // P):
+            span = slice(mt * S, (mt + 1) * S)
+            nc.scalar.activation(rden[:, mt, :], den_rows[:, span], ACT.Abs_reciprocal_sqrt)
+            inv_den = sb(f"inv_den{mt}", [P, S], F32)
+            nc.scalar.activation(inv_den[:], rden[:, mt, :], ACT.Square)
+            for u in (2 * mt, 2 * mt + 1):
+                nc.vector.tensor_tensor(dif[u][:], kr[u][:], pab[u][:], ALU.mult)
+            for u in (2 * mt, 2 * mt + 1):
+                nc.vector.tensor_tensor(num[:, u, :], dif[u][:, 0, :], dif[u][:, 1, :], ALU.add)
+            res = sb(f"res{mt}", [P, S], F32)
+            nc.vector.tensor_tensor(res[:], num_rows[:, span], inv_den[:], ALU.mult)
+            nc.sync.dma_start(out[mt * P : (mt + 1) * P, :], res[:])

@@ -1,6 +1,7 @@
 from contextlib import ExitStack
 
 import concourse.mybir as mybir
+from concourse.masks import make_identity
 
 K, T, S, N, H = 512, 2048, 512, 512, 512
 FLOPS = 2 * S * (K * H + H * N + K * N)
@@ -17,8 +18,13 @@ ALU = mybir.AluOpType
 
 P = 128
 PACK = 4
+BLOCKS = K // 32
+TILES = N // P
 HALF = S // 2
-Z_CHUNKS = ((0, 256), (256, 384), (384, 512))
+LINE = 4
+Z_RANGES = ((0, 256), (256, 384), (384, 512))
+LAST = Z_RANGES[-1][0]
+STEPS = ((0, 0, HALF), (0, HALF, S), (1, 0, S), (2, 0, S), (3, 0, HALF), (3, HALF, S))
 
 
 def tile_picked_mixhnormkern_none_p_kernel(tc, x_words, x_scales, w1, gn, w2, w3, offs, n1, hz, n2, n3, out):
@@ -27,8 +33,8 @@ def tile_picked_mixhnormkern_none_p_kernel(tc, x_words, x_scales, w1, gn, w2, w3
         keep = ctx.enter_context(tc.tile_pool(name="keep", bufs=1))
         psum = ctx.enter_context(tc.psum_pool(name="psum", bufs=1))
 
-        def sb(name, shape, dtype, tag=None):
-            return keep.tile(shape, dtype, name=name, tag=tag or name, align_bytes=64)
+        def sb(name, shape, dtype, after=None):
+            return keep.tile(shape, dtype, name=name, tag=after or name, align_bytes=64)
 
         def load_list(name, src):
             tile = sb(name, [P, S // 16], U16)
@@ -38,170 +44,188 @@ def tile_picked_mixhnormkern_none_p_kernel(tc, x_words, x_scales, w1, gn, w2, w3
         def entries(lst, lo, hi):
             return lst[:, lo // 16 : hi // 16]
 
+        def load_weight(name, src, after=None):
+            raw = sb(name, [P, PACK, N], F32, after)
+            nc.sync.dma_start(raw[:], src.rearrange("(p j) c -> p j c", j=PACK))
+            return raw
+
+        def quantise(codes, scales, values):
+            nc.vector.quantize_mx(out=codes.bitcast(FP8X4), scales=scales, in_=values)
+
+        def mx_pass(dst, w_codes, w_scales, mt, codes, scales, lo, hi, start, stop):
+            m = slice(mt * P, (mt + 1) * P)
+            nc.tensor.matmul_mx(out=dst, lhsT=w_codes[:, m].bitcast(FP8X4), lhsT_scale=w_scales[:, m],
+                                rhs=codes[:, lo:hi].bitcast(FP8X4), rhs_scale=scales[:, lo:hi], start=start, stop=stop)
+
         xs = sb("xs", [P, T], U8)
-        nc.vector.memset(xs[:].bitcast(I32), 0)
-        scale_rows = x_scales[0].bitcast(I32)
-        xs8 = sb("xs8", [P, T], U8)
-        nc.vector.memset(xs8[:].bitcast(I32), 0)
-        xh_s = sb("xh_s", [P, S], U8)
-        nc.vector.memset(xh_s[:].bitcast(I32), 0)
+        nc.sync.dma_start(xs[:].bitcast(I32), x_scales[0].bitcast(I32).unsqueeze(1).to_broadcast([BLOCKS, P // BLOCKS, T // 4]))
         offs_l = load_list("offs_l", offs)
         hz_l = load_list("hz_l", hz)
+        xw = sb("xw", [P, T], U32)
+        nc.sync.dma_start(xw[:].bitcast(I32), x_words[0].rearrange("p n t -> p (n t)").bitcast(I32))
         n1_l = load_list("n1_l", n1)
         n2_l = load_list("n2_l", n2)
         n3_l = load_list("n3_l", n3)
+        w1_raw = load_weight("w1_raw", w1)
         gain = sb("gain", [P, PACK], F32)
-        nc.sync.dma_start(gain[:], gn.rearrange("(p t) o -> p (t o)", t=PACK))
-        xw = sb("xw", [P, T], U32)
-        nc.sync.dma_start(xw[:].bitcast(I32), x_words[0].rearrange("p n t -> p (n t)").bitcast(I32))
-        for r in range(4):
-            nc.scalar.dma_start(xs[r:P:32, :].bitcast(I32), scale_rows[r:16:4, :])
-        nc.scalar.dma_start(xs8[0:P:8, :].bitcast(I32), scale_rows)
-        w1_rows = w1.rearrange("(p j) c -> p j c", j=PACK)
-        w1_raw = []
-        for c in range(2):
-            raw = sb(f"w1_raw{c}", [P, PACK, HALF], F32)
-            nc.sync.dma_start(raw[:], w1_rows[:, :, c * HALF : (c + 1) * HALF])
-            w1_raw.append(raw)
+        nc.gpsimd.dma_start(gain[:], gn.rearrange("(p t) o -> p (t o)", t=PACK))
 
+        x_planes = sb("x_planes", [P, 2 * S], U8)
+        nc.vector.memset(x_planes[:].bitcast(I32), 0)
         half = sb("half", [P, 1], F32)
         nc.vector.memset(half[:], 0.5)
+        ident = sb("ident", [P, P], F32)
+        make_identity(nc, ident[:])
+        warm = sb("warm", [P, 2], F32)
+        nc.scalar.activation(warm[:, 0:1], half[:], ACT.Abs_reciprocal_sqrt)
 
-        xq_s = sb("xq_s", [P, S], U8)
-        nc.vector.tensor_copy(xq_s[:], xs[:].indirect(offs_l[:]))
+        picked_s = sb("picked_s", [P, 2 * S], U8)
+        nc.vector.tensor_copy(picked_s[:, :S], xs[:].indirect(offs_l[:]))
+        nc.vector.tensor_copy(picked_s[:, S:], xs[:].indirect(hz_l[:]))
+        for r in range(4):
+            nc.sync.dma_start(x_planes[r:P:32, :].bitcast(I32), picked_s[8 * r : P : 32, :].bitcast(I32))
+        xq_s, xh_s = x_planes[:, :S], x_planes[:, S:]
         xq_w = sb("xq_w", [P, S], U32)
         nc.vector.tensor_copy(xq_w[:], xw[:].indirect(offs_l[:]))
         xh_w = sb("xh_w", [P, S], U32)
         nc.vector.tensor_copy(xh_w[:], xw[:].indirect(hz_l[:]))
+        w3_raw = load_weight("w3_raw", w3, after="xs")
+        w2_raw = load_weight("w2_raw", w2, after="xw")
 
         w1_b = sb("w1_b", [P, H * PACK], BF16)
         w1_dst = w1_b[:].rearrange("p (t m j) -> p m t j", t=PACK, j=PACK)
-        for c in range(2):
-            src = w1_raw[c][:].rearrange("p j (m t) -> p m t j", t=PACK)
-            dst = w1_dst[:, c * 64 : (c + 1) * 64]
-            if c == 0:
-                nc.scalar.copy(dst, src)
-            else:
-                nc.vector.tensor_copy(dst, src)
-        w3_raw = sb("w3_raw", [P, PACK, N], F32, tag="w1_raw0")
-        nc.sync.dma_start(w3_raw[:], w3.rearrange("(p j) c -> p j c", j=PACK))
-        w2_raw = sb("w2_raw", [P, PACK, N], F32, tag="w1_raw1")
-        nc.sync.dma_start(w2_raw[:], w2.rearrange("(p j) c -> p j c", j=PACK))
+        w1_src = w1_raw[:].rearrange("p j (m t) -> p m t j", t=PACK)
+        nc.scalar.copy(w1_dst[:, : P // 2], w1_src[:, : P // 2])
+        nc.vector.tensor_copy(w1_dst[:, P // 2 :], w1_src[:, P // 2 :])
         w1_c = sb("w1_c", [P, H], U32)
         w1_s = sb("w1_s", [P, H], U8)
-        y = [psum.tile([P, S], F32, name=f"y{t}") for t in range(PACK)]
-        for t in range(PACK):
-            m = slice(t * P, (t + 1) * P)
-            nc.vector.quantize_mx(out=w1_c[:, m].bitcast(FP8X4), scales=w1_s[:, m], in_=w1_b[:, t * P * PACK : (t + 1) * P * PACK])
-            nc.tensor.matmul_mx(out=y[t][:], lhsT=w1_c[:, m].bitcast(FP8X4), lhsT_scale=w1_s[:, m],
-                                rhs=xq_w[:].bitcast(FP8X4), rhs_scale=xq_s[:], start=True, stop=True)
+        for lo in range(0, H, H // 2):
+            quantise(w1_c[:, lo : lo + H // 2], w1_s[:, lo : lo + H // 2], w1_b[:, lo * PACK : (lo + H // 2) * PACK])
+        y = [psum.tile([P, PACK, P], F32, name=f"y{b}", tag=f"y{b}") for b in range(S // P)]
+        for b in range(S // P):
+            for t in range(PACK):
+                mx_pass(y[b][:, t, :], w1_c, w1_s, t, xq_w, xq_s, b * P, (b + 1) * P, True, True)
 
-        xh_raw = sb("xh_raw", [P, S], U8, tag="w1_b")
-        nc.vector.tensor_copy(xh_raw[:], xs8[:].indirect(hz_l[:]))
-        for r in range(4):
-            nc.sync.dma_start(xh_s[r:P:32, :].bitcast(I32), xh_raw[8 * r : P : 32, :].bitcast(I32))
+        def round_weight(name, raw):
+            grouped = sb(name, [P, N, PACK], BF16)
+            nc.vector.tensor_copy(grouped[:].rearrange("p (c i) j -> p c j i", i=LINE), raw[:].rearrange("p j (c i) -> p c j i", i=LINE))
+            return grouped[:].rearrange("p c j -> p (c j)")
 
-        def group_weight(name, raw, engine):
-            grouped = sb(name + "_b", [P, N, PACK], BF16)
-            dst = grouped[:].rearrange("p (c i) j -> p c j i", i=4)
-            src = raw[:].rearrange("p j (c i) -> p c j i", i=4)
-            if engine == "gpsimd":
-                nc.gpsimd.tensor_scalar(dst, src, 1.0, 0.0, ALU.mult, ALU.add)
-            else:
-                nc.vector.tensor_copy(dst, src)
-            return grouped
-
-        def quantise_weight(name, grouped):
-            codes = sb(name + "_c", [P, N], U32)
-            scales = sb(name + "_s", [P, N], U8)
-            nc.vector.quantize_mx(out=codes[:].bitcast(FP8X4), scales=scales[:], in_=grouped[:].rearrange("p c j -> p (c j)"))
-            return codes, scales
+        w3_c, w3_s = sb("w3_c", [P, N], U32), sb("w3_s", [P, N], U8)
+        w2_c, w2_s = sb("w2_c", [P, N], U32), sb("w2_s", [P, N], U8)
+        quantise(w3_c[:], w3_s[:], round_weight("w3_b", w3_raw))
+        w2_b = round_weight("w2_b", w2_raw)
 
         mag = sb("mag", [P, PACK, S], F32)
         root = sb("root", [P, PACK, S], F32)
-        inv = [sb(f"inv{t}", [P, S], F32) for t in range(PACK)]
-        w3_b = group_weight("w3", w3_raw, "vector")
+        inv = [sb(f"inv{t}", [P, S], F32, after="xw" if t == 0 else None) for t in range(PACK)]
+        for b in range(S // P):
+            nc.scalar.activation(mag[:, :, b * P : (b + 1) * P], y[b][:], ACT.Abs)
         for t in range(PACK):
-            nc.scalar.activation(mag[:, t, :], y[t][:], ACT.Abs)
             nc.scalar.activation(root[:, t, :], mag[:, t, :], ACT.Abs_reciprocal_sqrt, bias=half[:])
-            if t in (2, 3):
-                nc.scalar.activation(inv[t][:], root[:, t, :], ACT.Square)
-            else:
-                nc.vector.tensor_tensor(inv[t][:], root[:, t, :], root[:, t, :], ALU.mult)
-        w3_c, w3_s = quantise_weight("w3", w3_b)
-        h = [psum.tile([P, S], F32, name=f"h{m}") for m in range(N // P)]
-        for mt in range(N // P):
-            m = slice(mt * P, (mt + 1) * P)
-            nc.tensor.matmul_mx(out=h[mt][:], lhsT=w3_c[:, m].bitcast(FP8X4), lhsT_scale=w3_s[:, m],
-                                rhs=xh_w[:].bitcast(FP8X4), rhs_scale=xh_s[:], start=True, stop=False)
-        w2_c, w2_s = quantise_weight("w2", group_weight("w2", w2_raw, "vector"))
+            nc.vector.scalar_tensor_tensor(inv[t][:], root[:, t, :], gain[:, t : t + 1], root[:, t, :], ALU.mult, ALU.mult)
+        quantise(w2_c[:], w2_s[:], w2_b)
 
+        h = [psum.tile([P, LAST], F32, name=f"h{mt}", tag=f"h{mt}") for mt in range(TILES)]
+        for mt in range(TILES):
+            for lo, hi in Z_RANGES[:-1]:
+                mx_pass(h[mt][:, lo:hi], w3_c, w3_s, mt, xh_w, xh_s, lo, hi, lo == 0, False)
         z_c = sb("z_c", [P, S], U32)
         z_s = sb("z_s", [P, S], U8)
-        for lo, hi in Z_CHUNKS:
-            z_planes = sb(f"z_planes{lo}", [P, PACK, hi - lo], BF16)
+        got = (sb("got0", [P, PACK, HALF], F32), sb("got1", [P, PACK, HALF], F32, after="root"))
+
+        def looked_up(lo, hi):
+            return got[lo // HALF][:, :, lo % HALF : lo % HALF + hi - lo]
+
+        def make_z(lo, hi):
             for t in range(PACK):
-                got = sb(f"got{lo}_{t}", [P, hi - lo], F32)
-                nc.scalar.activation(got[:], inv[t][:].indirect(entries(n1_l, lo, hi)), ACT.Copy)
-                nc.vector.scalar_tensor_tensor(z_planes[:, t, :], y[t][:, lo:hi], gain[:, t : t + 1], got[:], ALU.mult, ALU.mult)
-            z_b = sb(f"z_b{lo}", [P, hi - lo, PACK], BF16)
-            nc.vector.tensor_copy(z_b[:].rearrange("p (c i) j -> p c j i", i=4), z_planes[:].rearrange("p j (c i) -> p c j i", i=4))
-            nc.vector.quantize_mx(out=z_c[:, lo:hi].bitcast(FP8X4), scales=z_s[:, lo:hi], in_=z_b[:].rearrange("p c j -> p (c j)"))
-            for mt in range(N // P):
-                m = slice(mt * P, (mt + 1) * P)
-                nc.tensor.matmul_mx(out=h[mt][:, lo:hi], lhsT=w2_c[:, m].bitcast(FP8X4), lhsT_scale=w2_s[:, m],
-                                    rhs=z_c[:, lo:hi].bitcast(FP8X4), rhs_scale=z_s[:, lo:hi], start=False, stop=(hi == S))
+                nc.scalar.activation(looked_up(lo, hi)[:, t, :], inv[t][:].indirect(entries(n1_l, lo, hi)), ACT.Copy)
+            z_b = sb(f"z_b{lo}", [P, hi - lo, PACK], BF16, after="w2_b")
+            for c in range(lo, hi, P):
+                nc.vector.tensor_tensor(z_b[:, c - lo : c - lo + P, :].rearrange("p (c i) t -> p c t i", i=LINE),
+                                        y[c // P][:].rearrange("p t (c i) -> p c t i", i=LINE),
+                                        looked_up(c, c + P).rearrange("p t (c i) -> p c t i", i=LINE), ALU.mult)
+            quantise(z_c[:, lo:hi], z_s[:, lo:hi], z_b[:].rearrange("p c j -> p (c j)"))
 
-        hs = [sb(f"hs{mt}", [P, S], F32) for mt in range(N // P)]
-        nc.scalar.copy(hs[0][:], h[0][:])
-        for mt in range(1, N // P):
-            nc.vector.tensor_copy(hs[mt][:], h[mt][:])
-        units = [(mt, c * HALF) for mt in range(N // P) for c in range(2)]
-        pab = [sb(f"pab{u}", [P, 2, HALF], F32) for u in range(len(units))]
-        dif = [sb(f"dif{u}", [P, 2, HALF], F32) for u in range(len(units))]
-        sq = [sb(f"sq{u}", [P, 4, P], F32)[:] for u in range(len(units) - 1)]
-        rden = sb("rden", [P, N // P, S], F32)
+        def add_z(lo, hi):
+            make_z(lo, hi)
+            for mt in range(TILES):
+                mx_pass(h[mt][:, lo:hi], w2_c, w2_s, mt, z_c, z_s, lo, hi, False, hi == LAST)
+
+        add_z(*Z_RANGES[0])
+        h_last = psum.tile([P, TILES, S - LAST], F32, name="h_last", tag="y0")
+        for mt in range(TILES):
+            mx_pass(h_last[:, mt, :], w3_c, w3_s, mt, xh_w, xh_s, LAST, S, mt == 0, False)
+        add_z(*Z_RANGES[1])
+        make_z(LAST, S)
+        for mt in range(TILES):
+            mx_pass(h_last[:, mt, :], w2_c, w2_s, mt, z_c, z_s, LAST, S, False, mt == TILES - 1)
+        nc.scalar.activation(warm[:, 1:2], got[1][:, PACK - 1, HALF - 1 : HALF], ACT.Exp, scale=-1.0)
+
+        hs = [sb(f"hs{mt}", [P, S], F32, after=(None, "w2_b", "z_s", "z_c")[mt]) for mt in range(TILES)]
+        nc.scalar.copy(hs[0][:, :LAST], h[0][:])
+        for mt in range(TILES):
+            nc.vector.tensor_copy(hs[mt][:, LAST:], h_last[:, mt, :])
+            if mt > 0:
+                nc.vector.tensor_copy(hs[mt][:, :LAST], h[mt][:])
+
+        pab = [sb(f"pab{mt}", [P, 2, S], F32) for mt in range(TILES)]
+        dif = [sb(f"dif{mt}", [P, 2, S], F32) for mt in range(TILES)]
+        kr = [sb(f"kr{mt}", [P, 2, S], F32) for mt in range(TILES)]
+        for mt in range(TILES):
+            for lo in (0, HALF):
+                for i, lst in enumerate((n2_l, n3_l)):
+                    nc.scalar.activation(pab[mt][:, i, lo : lo + HALF], hs[mt][:].indirect(entries(lst, lo, lo + HALF)), ACT.Copy)
+        rden = sb("rden", [P, TILES, S], F32)
+        sq = [sb(f"sq{u}", [P, 4, (hi - lo) // 2], F32)[:] for u, (mt, lo, hi) in enumerate(STEPS[:-1])]
         sq.append(rden[:, :, 0:P])
-        kr = [sb(f"kr{u}", [P, 2, HALF], F32) for u in range(len(units))]
-        den = sb("den", [P, len(units), HALF], F32)
-        num = sb("num", [P, len(units), HALF], F32)
+        den = [psum.tile([P, S], F32, name=f"den{mt}", tag=f"y{mt}") for mt in range(TILES)]
 
-        def fetch(u):
-            mt, lo = units[u]
-            for i, lst in enumerate((n2_l, n3_l)):
-                nc.scalar.activation(pab[u][:, i, :], hs[mt][:].indirect(entries(lst, lo, lo + HALF)), ACT.Copy)
+        def in_four(tile, lo, hi):
+            return tile[:, :, lo:hi].rearrange("p i (a c) -> p i a c", a=2)
+
+        def squares(u):
+            return sq[u].rearrange("p (i a) c -> p i a c", a=2)
 
         def differ(u):
-            mt, lo = units[u]
-            nc.vector.tensor_tensor(dif[u][:], pab[u][:], hs[mt][:, lo : lo + HALF].unsqueeze(1).to_broadcast([P, 2, HALF]), ALU.subtract)
+            mt, lo, hi = STEPS[u]
+            both = hs[mt][:, lo:hi].unsqueeze(1).to_broadcast([P, 2, hi - lo])
+            nc.vector.tensor_tensor(dif[mt][:, :, lo:hi], pab[mt][:, :, lo:hi], both, ALU.subtract)
 
         def square(u):
-            d4 = dif[u][:].rearrange("p i (a c) -> p (i a) c", a=2)
-            nc.vector.tensor_tensor(sq[u], d4, d4, ALU.mult)
+            mt, lo, hi = STEPS[u]
+            nc.vector.tensor_tensor(squares(u), in_four(dif[mt], lo, hi), in_four(dif[mt], lo, hi), ALU.mult)
 
         def weigh(u):
-            nc.scalar.activation(kr[u][:].rearrange("p i (a c) -> p (i a) c", a=2), sq[u], ACT.Exp, scale=-0.5)
+            mt, lo, hi = STEPS[u]
+            nc.scalar.activation(in_four(kr[mt], lo, hi), squares(u), ACT.Exp, scale=-0.5)
 
         def total(u):
-            nc.vector.scalar_tensor_tensor(den[:, u, :], kr[u][:, 0, :], 0.5, kr[u][:, 1, :], ALU.add, ALU.add)
+            mt, lo, hi = STEPS[u]
+            for c in range(lo, hi, P):
+                for i in range(2):
+                    nc.tensor.matmul(den[mt][:, c : c + P], kr[mt][:, i, c : c + P], ident[:], start=(i == 0), stop=(i == 1), is_transpose=True)
 
-        stages = (fetch, differ, square, weigh, total)
-        for step in range(len(units) + len(stages) - 1):
+        stages = (differ, square, weigh, total)
+        for step in range(len(STEPS) + len(stages) - 1):
             for lag, stage in enumerate(stages):
-                if 0 <= step - lag < len(units):
+                if 0 <= step - lag < len(STEPS):
                     stage(step - lag)
 
-        num_rows = num[:].rearrange("p u c -> p (u c)")
-        den_rows = den[:].rearrange("p u c -> p (u c)")
-        for mt in range(N // P):
-            span = slice(mt * S, (mt + 1) * S)
-            nc.scalar.activation(rden[:, mt, :], den_rows[:, span], ACT.Abs_reciprocal_sqrt)
-            inv_den = sb(f"inv_den{mt}", [P, S], F32)
-            nc.scalar.activation(inv_den[:], rden[:, mt, :], ACT.Square)
-            for u in (2 * mt, 2 * mt + 1):
-                nc.vector.tensor_tensor(dif[u][:], kr[u][:], pab[u][:], ALU.mult)
-            for u in (2 * mt, 2 * mt + 1):
-                nc.vector.tensor_tensor(num[:, u, :], dif[u][:, 0, :], dif[u][:, 1, :], ALU.add)
-            res = sb(f"res{mt}", [P, S], F32)
-            nc.vector.tensor_tensor(res[:], num_rows[:, span], inv_den[:], ALU.mult)
-            nc.sync.dma_start(out[mt * P : (mt + 1) * P, :], res[:])
+        num = [sb(f"num{mt}", [P, S], F32) for mt in range(TILES)]
+        for mt in range(TILES + 1):
+            if mt < TILES:
+                nc.vector.tensor_tensor(dif[mt][:], kr[mt][:], pab[mt][:], ALU.mult)
+            if mt > 0:
+                nc.vector.tensor_tensor(num[mt - 1][:], dif[mt - 1][:, 0, :], dif[mt - 1][:, 1, :], ALU.add)
+        spans = [(mt, 0, S) for mt in range(TILES - 1)] + [(TILES - 1, 0, HALF), (TILES - 1, HALF, S)]
+        inv_den = sb("inv_den", [P, TILES, S], F32)
+        res = sb("res", [P, TILES, S], F32)
+        for n, (mt, lo, hi) in enumerate(spans):
+            nc.scalar.activation(rden[:, mt, lo:hi], den[mt][:, lo:hi], ACT.Abs_reciprocal_sqrt, bias=half[:])
+            nc.scalar.activation(inv_den[:, mt, lo:hi], rden[:, mt, lo:hi], ACT.Square)
+            back = psum.tile([P, hi - lo], F32, name=f"back{n}", tag=f"h{n % TILES}")
+            for c in range(lo, hi, P):
+                nc.tensor.transpose(back[:, c - lo : c - lo + P], inv_den[:, mt, c : c + P], ident[:])
+            nc.vector.tensor_tensor(res[:, mt, lo:hi], num[mt][:, lo:hi], back[:], ALU.mult)
+            nc.sync.dma_start(out[mt * P : (mt + 1) * P, lo:hi], res[:, mt, lo:hi])

@@ -23,7 +23,7 @@ TILES = N // P
 HALF = S // 2
 LINE = 4
 Z_RANGES = ((0, 256), (256, 384), (384, 512))
-LAST = Z_RANGES[-1][0]
+W1_ON_SCALAR = 48
 STEPS = ((0, 0, HALF), (0, HALF, S), (1, 0, S), (2, 0, S), (3, 0, HALF), (3, HALF, S))
 
 
@@ -95,8 +95,8 @@ def tile_picked_mixhnormkern_none_p_kernel(tc, x_words, x_scales, w1, gn, w2, w3
         w1_b = sb("w1_b", [P, H * PACK], BF16)
         w1_dst = w1_b[:].rearrange("p (t m j) -> p m t j", t=PACK, j=PACK)
         w1_src = w1_raw[:].rearrange("p j (m t) -> p m t j", t=PACK)
-        nc.scalar.copy(w1_dst[:, : P // 2], w1_src[:, : P // 2])
-        nc.vector.tensor_copy(w1_dst[:, P // 2 :], w1_src[:, P // 2 :])
+        nc.scalar.copy(w1_dst[:, :W1_ON_SCALAR], w1_src[:, :W1_ON_SCALAR])
+        nc.vector.tensor_copy(w1_dst[:, W1_ON_SCALAR:], w1_src[:, W1_ON_SCALAR:])
         w1_c = sb("w1_c", [P, H], U32)
         w1_s = sb("w1_s", [P, H], U8)
         for lo in range(0, H, H // 2):
@@ -126,10 +126,9 @@ def tile_picked_mixhnormkern_none_p_kernel(tc, x_words, x_scales, w1, gn, w2, w3
             nc.vector.scalar_tensor_tensor(inv[t][:], root[:, t, :], gain[:, t : t + 1], root[:, t, :], ALU.mult, ALU.mult)
         quantise(w2_c[:], w2_s[:], w2_b)
 
-        h = [psum.tile([P, LAST], F32, name=f"h{mt}", tag=f"h{mt}") for mt in range(TILES)]
+        h = [psum.tile([P, S], F32, name=f"h{mt}", tag=f"h{mt}") for mt in range(TILES)]
         for mt in range(TILES):
-            for lo, hi in Z_RANGES[:-1]:
-                mx_pass(h[mt][:, lo:hi], w3_c, w3_s, mt, xh_w, xh_s, lo, hi, lo == 0, False)
+            mx_pass(h[mt][:], w3_c, w3_s, mt, xh_w, xh_s, 0, S, True, False)
         z_c = sb("z_c", [P, S], U32)
         z_s = sb("z_s", [P, S], U8)
         got = (sb("got0", [P, PACK, HALF], F32), sb("got1", [P, PACK, HALF], F32, after="root"))
@@ -137,7 +136,7 @@ def tile_picked_mixhnormkern_none_p_kernel(tc, x_words, x_scales, w1, gn, w2, w3
         def looked_up(lo, hi):
             return got[lo // HALF][:, :, lo % HALF : lo % HALF + hi - lo]
 
-        def make_z(lo, hi):
+        for lo, hi in Z_RANGES:
             for t in range(PACK):
                 nc.scalar.activation(looked_up(lo, hi)[:, t, :], inv[t][:].indirect(entries(n1_l, lo, hi)), ACT.Copy)
             z_b = sb(f"z_b{lo}", [P, hi - lo, PACK], BF16, after="w2_b")
@@ -146,28 +145,14 @@ def tile_picked_mixhnormkern_none_p_kernel(tc, x_words, x_scales, w1, gn, w2, w3
                                         y[c // P][:].rearrange("p t (c i) -> p c t i", i=LINE),
                                         looked_up(c, c + P).rearrange("p t (c i) -> p c t i", i=LINE), ALU.mult)
             quantise(z_c[:, lo:hi], z_s[:, lo:hi], z_b[:].rearrange("p c j -> p (c j)"))
-
-        def add_z(lo, hi):
-            make_z(lo, hi)
             for mt in range(TILES):
-                mx_pass(h[mt][:, lo:hi], w2_c, w2_s, mt, z_c, z_s, lo, hi, False, hi == LAST)
-
-        add_z(*Z_RANGES[0])
-        h_last = psum.tile([P, TILES, S - LAST], F32, name="h_last", tag="y0")
-        for mt in range(TILES):
-            mx_pass(h_last[:, mt, :], w3_c, w3_s, mt, xh_w, xh_s, LAST, S, mt == 0, False)
-        add_z(*Z_RANGES[1])
-        make_z(LAST, S)
-        for mt in range(TILES):
-            mx_pass(h_last[:, mt, :], w2_c, w2_s, mt, z_c, z_s, LAST, S, False, mt == TILES - 1)
+                mx_pass(h[mt][:, lo:hi], w2_c, w2_s, mt, z_c, z_s, lo, hi, False, hi == S)
         nc.scalar.activation(warm[:, 1:2], got[1][:, PACK - 1, HALF - 1 : HALF], ACT.Exp, scale=-1.0)
 
-        hs = [sb(f"hs{mt}", [P, S], F32, after=(None, "w2_b", "z_s", "z_c")[mt]) for mt in range(TILES)]
-        nc.scalar.copy(hs[0][:, :LAST], h[0][:])
-        for mt in range(TILES):
-            nc.vector.tensor_copy(hs[mt][:, LAST:], h_last[:, mt, :])
-            if mt > 0:
-                nc.vector.tensor_copy(hs[mt][:, :LAST], h[mt][:])
+        hs = [sb(f"hs{mt}", [P, S], F32) for mt in range(TILES)]
+        nc.scalar.copy(hs[0][:], h[0][:])
+        for mt in range(1, TILES):
+            nc.vector.tensor_copy(hs[mt][:], h[mt][:])
 
         pab = [sb(f"pab{mt}", [P, 2, S], F32) for mt in range(TILES)]
         dif = [sb(f"dif{mt}", [P, 2, S], F32) for mt in range(TILES)]

@@ -61,12 +61,12 @@ def tile_picked_mixhnormkern_none_p_kernel(tc, x_words, x_scales, w1, gn, w2, w3
         nc.sync.dma_start(xs[:].bitcast(I32), x_scales[0].bitcast(I32).unsqueeze(1).to_broadcast([BLOCKS, P // BLOCKS, T // 4]))
         offs_l = load_list("offs_l", offs)
         hz_l = load_list("hz_l", hz)
-        xw = sb("xw", [P, T], U32)
-        nc.sync.dma_start(xw[:].bitcast(I32), x_words[0].rearrange("p n t -> p (n t)").bitcast(I32))
+        w1_raw = load_weight("w1_raw", w1)
         n1_l = load_list("n1_l", n1)
         n2_l = load_list("n2_l", n2)
         n3_l = load_list("n3_l", n3)
-        w1_raw = load_weight("w1_raw", w1)
+        xw = sb("xw", [P, T], U32)
+        nc.sync.dma_start(xw[:].bitcast(I32), x_words[0].rearrange("p n t -> p (n t)").bitcast(I32))
         gain = sb("gain", [P, PACK], F32)
         nc.gpsimd.dma_start(gain[:], gn.rearrange("(p t) o -> p (t o)", t=PACK))
 
@@ -85,22 +85,23 @@ def tile_picked_mixhnormkern_none_p_kernel(tc, x_words, x_scales, w1, gn, w2, w3
         for r in range(4):
             nc.sync.dma_start(x_planes[r:P:32, :].bitcast(I32), picked_s[8 * r : P : 32, :].bitcast(I32))
         xq_s, xh_s = x_planes[:, :S], x_planes[:, S:]
-        xq_w = sb("xq_w", [P, S], U32)
-        nc.vector.tensor_copy(xq_w[:], xw[:].indirect(offs_l[:]))
-        xh_w = sb("xh_w", [P, S], U32)
-        nc.vector.tensor_copy(xh_w[:], xw[:].indirect(hz_l[:]))
         w3_raw = load_weight("w3_raw", w3, after="xs")
-        w2_raw = load_weight("w2_raw", w2, after="xw")
 
         w1_b = sb("w1_b", [P, H * PACK], BF16)
         w1_dst = w1_b[:].rearrange("p (t m j) -> p m t j", t=PACK, j=PACK)
         w1_src = w1_raw[:].rearrange("p j (m t) -> p m t j", t=PACK)
         nc.scalar.copy(w1_dst[:, :W1_ON_SCALAR], w1_src[:, :W1_ON_SCALAR])
         nc.vector.tensor_copy(w1_dst[:, W1_ON_SCALAR:], w1_src[:, W1_ON_SCALAR:])
+        w2_raw = load_weight("w2_raw", w2, after="w1_raw")
         w1_c = sb("w1_c", [P, H], U32)
         w1_s = sb("w1_s", [P, H], U8)
         for lo in range(0, H, H // 2):
             quantise(w1_c[:, lo : lo + H // 2], w1_s[:, lo : lo + H // 2], w1_b[:, lo * PACK : (lo + H // 2) * PACK])
+        xq_w = sb("xq_w", [P, S], U32)
+        for lo in (0, HALF):
+            nc.vector.tensor_copy(xq_w[:, lo : lo + HALF], xw[:].indirect(entries(offs_l, lo, lo + HALF)))
+        xh_w = sb("xh_w", [P, S], U32)
+        nc.vector.tensor_copy(xh_w[:], xw[:].indirect(hz_l[:]))
         y = [psum.tile([P, PACK, P], F32, name=f"y{b}", tag=f"y{b}") for b in range(S // P)]
         for b in range(S // P):
             for t in range(PACK):
@@ -118,7 +119,7 @@ def tile_picked_mixhnormkern_none_p_kernel(tc, x_words, x_scales, w1, gn, w2, w3
 
         mag = sb("mag", [P, PACK, S], F32)
         root = sb("root", [P, PACK, S], F32)
-        inv = [sb(f"inv{t}", [P, S], F32, after="xw" if t == 0 else None) for t in range(PACK)]
+        inv = [sb(f"inv{t}", [P, S], F32) for t in range(PACK)]
         for b in range(S // P):
             nc.scalar.activation(mag[:, :, b * P : (b + 1) * P], y[b][:], ACT.Abs)
         for t in range(PACK):

from contextlib import ExitStack

import concourse.mybir as mybir
from concourse.masks import make_identity

K, T, S, N, H = 512, 2048, 512, 512, 512
FLOPS = 2 * S * (K * H + H * N + K * N)

F32 = mybir.dt.float32
BF16 = mybir.dt.bfloat16
I32 = mybir.dt.int32
U32 = mybir.dt.uint32
U16 = mybir.dt.uint16
U8 = mybir.dt.uint8
FP8X4 = mybir.dt.float8_e4m3fn_x4
ACT = mybir.ActivationFunctionType
ALU = mybir.AluOpType

P = 128
PACK = 4
BLOCKS = K // 32
TILES = N // P
HALF = S // 2
LINE = 4
Z_RANGES = ((0, 256), (256, 384), (384, 512))
W1_ON_SCALAR = 48
STEPS = ((0, 0, HALF), (0, HALF, S), (1, 0, S), (2, 0, S), (3, 0, HALF), (3, HALF, S))


def tile_picked_mixhnormkern_none_p_kernel(tc, x_words, x_scales, w1, gn, w2, w3, offs, n1, hz, n2, n3, out):
    nc = tc.nc
    with ExitStack() as ctx:
        keep = ctx.enter_context(tc.tile_pool(name="keep", bufs=1))
        psum = ctx.enter_context(tc.psum_pool(name="psum", bufs=1))

        def sb(name, shape, dtype, after=None):
            return keep.tile(shape, dtype, name=name, tag=after or name, align_bytes=64)

        def load_list(name, src):
            tile = sb(name, [P, S // 16], U16)
            nc.sync.dma_start(tile[:], src)
            return tile

        def entries(lst, lo, hi):
            return lst[:, lo // 16 : hi // 16]

        def load_weight(name, src, after=None):
            raw = sb(name, [P, PACK, N], F32, after)
            nc.sync.dma_start(raw[:], src.rearrange("(p j) c -> p j c", j=PACK))
            return raw

        def quantise(codes, scales, values):
            nc.vector.quantize_mx(out=codes.bitcast(FP8X4), scales=scales, in_=values)

        def mx_pass(dst, w_codes, w_scales, mt, codes, scales, lo, hi, start, stop):
            m = slice(mt * P, (mt + 1) * P)
            nc.tensor.matmul_mx(out=dst, lhsT=w_codes[:, m].bitcast(FP8X4), lhsT_scale=w_scales[:, m],
                                rhs=codes[:, lo:hi].bitcast(FP8X4), rhs_scale=scales[:, lo:hi], start=start, stop=stop)

        xs = sb("xs", [P, T], U8)
        nc.sync.dma_start(xs[:].bitcast(I32), x_scales[0].bitcast(I32).unsqueeze(1).to_broadcast([BLOCKS, P // BLOCKS, T // 4]))
        offs_l = load_list("offs_l", offs)
        hz_l = load_list("hz_l", hz)
        w1_raw = load_weight("w1_raw", w1)
        n1_l = load_list("n1_l", n1)
        n2_l = load_list("n2_l", n2)
        n3_l = load_list("n3_l", n3)
        xw = sb("xw", [P, T], U32)
        nc.sync.dma_start(xw[:].bitcast(I32), x_words[0].rearrange("p n t -> p (n t)").bitcast(I32))
        gain = sb("gain", [P, PACK], F32)
        nc.gpsimd.dma_start(gain[:], gn.rearrange("(p t) o -> p (t o)", t=PACK))

        x_planes = sb("x_planes", [P, 2 * S], U8)
        nc.vector.memset(x_planes[:].bitcast(I32), 0)
        half = sb("half", [P, 1], F32)
        nc.vector.memset(half[:], 0.5)
        ident = sb("ident", [P, P], F32)
        make_identity(nc, ident[:])
        warm = sb("warm", [P, 2], F32)
        nc.scalar.activation(warm[:, 0:1], half[:], ACT.Abs_reciprocal_sqrt)

        picked_s = sb("picked_s", [P, 2 * S], U8)
        nc.vector.tensor_copy(picked_s[:, :S], xs[:].indirect(offs_l[:]))
        nc.vector.tensor_copy(picked_s[:, S:], xs[:].indirect(hz_l[:]))
        for r in range(4):
            nc.sync.dma_start(x_planes[r:P:32, :].bitcast(I32), picked_s[8 * r : P : 32, :].bitcast(I32))
        xq_s, xh_s = x_planes[:, :S], x_planes[:, S:]
        w3_raw = load_weight("w3_raw", w3, after="xs")

        w1_b = sb("w1_b", [P, H * PACK], BF16)
        w1_dst = w1_b[:].rearrange("p (t m j) -> p m t j", t=PACK, j=PACK)
        w1_src = w1_raw[:].rearrange("p j (m t) -> p m t j", t=PACK)
        nc.scalar.copy(w1_dst[:, :W1_ON_SCALAR], w1_src[:, :W1_ON_SCALAR])
        nc.vector.tensor_copy(w1_dst[:, W1_ON_SCALAR:], w1_src[:, W1_ON_SCALAR:])
        w2_raw = load_weight("w2_raw", w2, after="w1_raw")
        w1_c = sb("w1_c", [P, H], U32)
        w1_s = sb("w1_s", [P, H], U8)
        for lo in range(0, H, H // 2):
            quantise(w1_c[:, lo : lo + H // 2], w1_s[:, lo : lo + H // 2], w1_b[:, lo * PACK : (lo + H // 2) * PACK])
        xq_w = sb("xq_w", [P, S], U32)
        for lo in (0, HALF):
            nc.vector.tensor_copy(xq_w[:, lo : lo + HALF], xw[:].indirect(entries(offs_l, lo, lo + HALF)))
        xh_w = sb("xh_w", [P, S], U32)
        nc.vector.tensor_copy(xh_w[:], xw[:].indirect(hz_l[:]))
        y = [psum.tile([P, PACK, P], F32, name=f"y{b}", tag=f"y{b}") for b in range(S // P)]
        for b in range(S // P):
            for t in range(PACK):
                mx_pass(y[b][:, t, :], w1_c, w1_s, t, xq_w, xq_s, b * P, (b + 1) * P, True, True)

        def round_weight(name, raw):
            grouped = sb(name, [P, N, PACK], BF16)
            nc.vector.tensor_copy(grouped[:].rearrange("p (c i) j -> p c j i", i=LINE), raw[:].rearrange("p j (c i) -> p c j i", i=LINE))
            return grouped[:].rearrange("p c j -> p (c j)")

        w3_c, w3_s = sb("w3_c", [P, N], U32), sb("w3_s", [P, N], U8)
        w2_c, w2_s = sb("w2_c", [P, N], U32), sb("w2_s", [P, N], U8)
        quantise(w3_c[:], w3_s[:], round_weight("w3_b", w3_raw))
        w2_b = round_weight("w2_b", w2_raw)

        mag = sb("mag", [P, PACK, S], F32)
        root = sb("root", [P, PACK, S], F32)
        inv = [sb(f"inv{t}", [P, S], F32) for t in range(PACK)]
        for b in range(S // P):
            nc.scalar.activation(mag[:, :, b * P : (b + 1) * P], y[b][:], ACT.Abs)
        for t in range(PACK):
            nc.scalar.activation(root[:, t, :], mag[:, t, :], ACT.Abs_reciprocal_sqrt, bias=half[:])
            nc.vector.scalar_tensor_tensor(inv[t][:], root[:, t, :], gain[:, t : t + 1], root[:, t, :], ALU.mult, ALU.mult)
        quantise(w2_c[:], w2_s[:], w2_b)

        h = [psum.tile([P, S], F32, name=f"h{mt}", tag=f"h{mt}") for mt in range(TILES)]
        for mt in range(TILES):
            mx_pass(h[mt][:], w3_c, w3_s, mt, xh_w, xh_s, 0, S, True, False)
        z_c = sb("z_c", [P, S], U32)
        z_s = sb("z_s", [P, S], U8)
        got = (sb("got0", [P, PACK, HALF], F32), sb("got1", [P, PACK, HALF], F32, after="root"))

        def looked_up(lo, hi):
            return got[lo // HALF][:, :, lo % HALF : lo % HALF + hi - lo]

        for lo, hi in Z_RANGES:
            for t in range(PACK):
                nc.scalar.activation(looked_up(lo, hi)[:, t, :], inv[t][:].indirect(entries(n1_l, lo, hi)), ACT.Copy)
            z_b = sb(f"z_b{lo}", [P, hi - lo, PACK], BF16, after="w2_b")
            for c in range(lo, hi, P):
                nc.vector.tensor_tensor(z_b[:, c - lo : c - lo + P, :].rearrange("p (c i) t -> p c t i", i=LINE),
                                        y[c // P][:].rearrange("p t (c i) -> p c t i", i=LINE),
                                        looked_up(c, c + P).rearrange("p t (c i) -> p c t i", i=LINE), ALU.mult)
            quantise(z_c[:, lo:hi], z_s[:, lo:hi], z_b[:].rearrange("p c j -> p (c j)"))
            for mt in range(TILES):
                mx_pass(h[mt][:, lo:hi], w2_c, w2_s, mt, z_c, z_s, lo, hi, False, hi == S)
        nc.scalar.activation(warm[:, 1:2], got[1][:, PACK - 1, HALF - 1 : HALF], ACT.Exp, scale=-1.0)

        hs = [sb(f"hs{mt}", [P, S], F32) for mt in range(TILES)]
        nc.scalar.copy(hs[0][:], h[0][:])
        for mt in range(1, TILES):
            nc.vector.tensor_copy(hs[mt][:], h[mt][:])

        pab = [sb(f"pab{mt}", [P, 2, S], F32) for mt in range(TILES)]
        dif = [sb(f"dif{mt}", [P, 2, S], F32) for mt in range(TILES)]
        kr = [sb(f"kr{mt}", [P, 2, S], F32) for mt in range(TILES)]
        for mt in range(TILES):
            for lo in (0, HALF):
                for i, lst in enumerate((n2_l, n3_l)):
                    nc.scalar.activation(pab[mt][:, i, lo : lo + HALF], hs[mt][:].indirect(entries(lst, lo, lo + HALF)), ACT.Copy)
        rden = sb("rden", [P, TILES, S], F32)
        sq = [sb(f"sq{u}", [P, 4, (hi - lo) // 2], F32)[:] for u, (mt, lo, hi) in enumerate(STEPS[:-1])]
        sq.append(rden[:, :, 0:P])
        den = [psum.tile([P, S], F32, name=f"den{mt}", tag=f"y{mt}") for mt in range(TILES)]

        def in_four(tile, lo, hi):
            return tile[:, :, lo:hi].rearrange("p i (a c) -> p i a c", a=2)

        def squares(u):
            return sq[u].rearrange("p (i a) c -> p i a c", a=2)

        def differ(u):
            mt, lo, hi = STEPS[u]
            both = hs[mt][:, lo:hi].unsqueeze(1).to_broadcast([P, 2, hi - lo])
            nc.vector.tensor_tensor(dif[mt][:, :, lo:hi], pab[mt][:, :, lo:hi], both, ALU.subtract)

        def square(u):
            mt, lo, hi = STEPS[u]
            nc.vector.tensor_tensor(squares(u), in_four(dif[mt], lo, hi), in_four(dif[mt], lo, hi), ALU.mult)

        def weigh(u):
            mt, lo, hi = STEPS[u]
            nc.scalar.activation(in_four(kr[mt], lo, hi), squares(u), ACT.Exp, scale=-0.5)

        def total(u):
            mt, lo, hi = STEPS[u]
            for c in range(lo, hi, P):
                for i in range(2):
                    nc.tensor.matmul(den[mt][:, c : c + P], kr[mt][:, i, c : c + P], ident[:], start=(i == 0), stop=(i == 1), is_transpose=True)

        stages = (differ, square, weigh, total)
        for step in range(len(STEPS) + len(stages) - 1):
            for lag, stage in enumerate(stages):
                if 0 <= step - lag < len(STEPS):
                    stage(step - lag)

        num = [sb(f"num{mt}", [P, S], F32) for mt in range(TILES)]
        for mt in range(TILES + 1):
            if mt < TILES:
                nc.vector.tensor_tensor(dif[mt][:], kr[mt][:], pab[mt][:], ALU.mult)
            if mt > 0:
                nc.vector.tensor_tensor(num[mt - 1][:], dif[mt - 1][:, 0, :], dif[mt - 1][:, 1, :], ALU.add)
        spans = [(mt, 0, S) for mt in range(TILES - 1)] + [(TILES - 1, 0, HALF), (TILES - 1, HALF, S)]
        inv_den = sb("inv_den", [P, TILES, S], F32)
        res = sb("res", [P, TILES, S], F32)
        for n, (mt, lo, hi) in enumerate(spans):
            nc.scalar.activation(rden[:, mt, lo:hi], den[mt][:, lo:hi], ACT.Abs_reciprocal_sqrt, bias=half[:])
            nc.scalar.activation(inv_den[:, mt, lo:hi], rden[:, mt, lo:hi], ACT.Square)
            back = psum.tile([P, hi - lo], F32, name=f"back{n}", tag=f"h{n % TILES}")
            for c in range(lo, hi, P):
                nc.tensor.transpose(back[:, c - lo : c - lo + P], inv_den[:, mt, c : c + P], ident[:])
            nc.vector.tensor_tensor(res[:, mt, lo:hi], num[mt][:, lo:hi], back[:], ALU.mult)
            nc.sync.dma_start(out[mt * P : (mt + 1) * P, lo:hi], res[:, mt, lo:hi])
